import numpy as np
import ml_dtypes


def mxq(x, axis, fmt="e4m3"):
    dtype, down = {"e4m3": (ml_dtypes.float8_e4m3fn, 7), "e5m2": (ml_dtypes.float8_e5m2, 14)}[fmt]
    v = np.moveaxis(np.asarray(x, np.float32).astype(ml_dtypes.bfloat16).astype(np.float64), axis, -1)
    blocks = v.reshape(v.shape[:-1] + (-1, 32))
    amax = np.abs(blocks).max(-1, keepdims=True)
    byte = np.maximum(np.where(amax > 0, np.frexp(amax)[1] - 1 + 127, 0) - down, 1)
    scale = np.exp2(byte - 127.0)
    codes = (blocks / scale).astype(np.float32).astype(dtype).astype(np.float64)
    return np.moveaxis((codes * scale).reshape(v.shape), -1, axis)


WIDE = False


def mx_kscale(k):
    if not WIDE:
        return np.ones(k)
    levels = np.array([10, -10, 5, -5, 0])
    if k % 512:
        return np.exp2(np.random.permutation(np.resize(levels, k // 32))).repeat(32)
    a = np.empty((k // 512, 16))
    for p in range(k // 512):
        a[p, :8] = np.random.permutation(np.resize(levels, 8))
        for g in range(8):
            far = levels[np.abs(levels - a[p, g]) >= 10]
            a[p, g + 8] = far[np.random.randint(len(far))]
    return np.exp2(a.ravel()).repeat(32)


BF16 = ml_dtypes.bfloat16


def bf(x):
    return np.asarray(x, np.float32).astype(BF16)


def f64(x):
    return np.asarray(x).astype(np.float64)


V, H, K, J, R = 4, 512, 1024, 1024, 512


def draw0():
    s, t = mx_kscale(K), mx_kscale(H)
    fade = np.exp(-2.0 * np.arange(H) / H)
    lasting = np.random.standard_normal((V, 1, K)) * fade[:, None]
    passing = 0.7 * np.random.standard_normal((V, H, K))
    size = np.random.uniform(0.5, 1.5, J)
    factor = np.random.standard_normal((K, J)) * size / np.sqrt(K)
    reach = (0.3 + np.tri(R, H)) * np.square(np.random.standard_normal((R, H)))
    return {"psi": bf((lasting + passing) * s * t[:, None]),
            "factor": bf(factor / s[:, None]),
            "cum": bf(reach / H / (t * t))}


def core(psi, factor, cum):
    theta = mxq(f64(psi), 2, "e4m3") @ mxq(f64(factor), 0, "e4m3")
    power = np.square(theta)
    var = mxq(f64(cum), 1, "e4m3") @ mxq(power, 1, "e4m3")
    level = np.mean(var, axis=2, keepdims=True)
    return var / level


def e4m3fn_bytes(y):
    return np.clip(np.asarray(y, np.float64), -448.0, 448.0).astype(np.float32).astype(ml_dtypes.float8_e4m3fn).view(np.uint8)


def e4m3fn_values(b):
    return np.asarray(b, np.uint8).view(ml_dtypes.float8_e4m3fn).astype(np.float64)


def setup_inputs():
    d = draw0()
    x0 = np.asarray(d['factor']).astype(np.float64)
    s = (np.max(np.abs(x0), axis=(1,), keepdims=True) / 448.0).astype(np.float32)
    out = {}
    for k, v in d.items():
        if k == 'factor':
            out['factor_bytes'] = e4m3fn_bytes(x0 / s.astype(np.float64))
            out['factor_scale'] = s
        else:
            out[k] = v
    return out


def reference(psi, factor_bytes, factor_scale, cum):
    return core(psi, e4m3fn_values(factor_bytes) * factor_scale.astype(np.float64), cum)

from contextlib import ExitStack

import concourse.mybir as mybir
from concourse.masks import make_identity

V, H, K, J, R = 4, 512, 1024, 1024, 512
FLOPS = 2 * V * (H * K * J + R * H * J)

F32 = mybir.dt.float32
BF16 = mybir.dt.bfloat16
U32 = mybir.dt.uint32
U8 = mybir.dt.uint8
FP8 = mybir.dt.float8_e4m3fn
FP8X4 = mybir.dt.float8_e4m3fn_x4
ACT = mybir.ActivationFunctionType
ALU = mybir.AluOpType
AX = mybir.AxisListType

P = 128
T = 4
G = K // (P * T)
CHUNK = 256
N_CHUNKS = J // CHUNK
N_UNIT = 128
UNITS = J // N_UNIT
HALF = 512
UNITS_PER_HALF = HALF // N_UNIT


CFG = {'chunks': [256, 256, 256, 256], 'fstep': [-1, -1, 0, 3], 'tr': {(1, 0): 4, (1, 1): -1, (1, 2): 1, (1, 3): 4, ('cum', 0): 1, ('cum', 1): 1, (2, 0): 2, (2, 1): 2, (2, 2): 4, (2, 3): 4, (3, 0): 4, (3, 1): 4, (3, 2): 8, (3, 3): 12}, 'cpv': [(3, 3), (2, 1)], 'pq': {1: 5, 2: 6, 3: 16}, 'cq': 1, 'sw': [(1, 0), (2, 0), (0, 0)], 'rv': [(2, 1), (3, 1), (4, 1), (5, 1), (3, 0), (6, 0), (5, 0), (1, 0), (0, 3), (0, 1), (1, 1), (4, 3), (0, 0)], 'lag2': 5, 'lagr': 1, 'red': [4, 6], 'nm': [4, 5, 6, 7], 'bufs': (3, 2, 3), 'sqf': 0
}


def tile_forecast_variance_shares_s7_kernel(tc, psi, factor_bytes, factor_scale, cum, out):
    nc = tc.nc
    with ExitStack() as ctx:
        keep = ctx.enter_context(tc.tile_pool(name="keep", bufs=1))
        pool = ctx.enter_context(tc.tile_pool(name="work", bufs=3))
        keep4 = ctx.enter_context(tc.tile_pool(name="psi", bufs=4))
        outs = ctx.enter_context(tc.tile_pool(name="outs", bufs=3))
        ps_t = ctx.enter_context(tc.psum_pool(name="ps_t", bufs=CFG["bufs"][0]))
        ps_a = ctx.enter_context(tc.psum_pool(name="ps_a", bufs=CFG["bufs"][1]))
        ps_b = ctx.enter_context(tc.psum_pool(name="ps_b", bufs=CFG["bufs"][2]))

        ident = keep.tile([P, P], F32, name="ident")
        make_identity(nc, ident[:])
        warm = keep.tile([P, 2], F32, name="warm")
        nc.vector.memset(warm[:], 1.0)

        ctx.enter_context(tc.manual_schedule())

        nc.scalar.activation(warm[:, 1:2], warm[:, 0:1], ACT.Square)

        fb = [keep.tile([P, G, T, 512], U8, name="fb%d" % h) for h in range(2)]
        fs = keep.tile([P, G * T], F32, name="fs")
        widths = CFG["chunks"]
        starts = [sum(widths[:c]) for c in range(len(widths))]
        fc = [keep.tile([P, G, n], U32, name="fc%d" % c, align_bytes=64) for c, n in enumerate(widths)]
        fsc = [keep.tile([P, G, n], U8, name="fsc%d" % c, align_bytes=64) for c, n in enumerate(widths)]
        cum_raw = keep.tile([P, T, H], BF16, name="cum_raw")
        cum_g = keep.tile([P, T * H], BF16, name="cum_g", align_bytes=64)
        cc = keep.tile([P, T, P], U32, name="cc", align_bytes=64)
        cs = keep.tile([P, T, P], U8, name="cs", align_bytes=64)
        psi_raw = [keep.tile([P, T, K], BF16, name="psi_raw%d" % v) for v in range(V)]

        nc.sync.dma_start(out=fs[:].rearrange("p (g t) -> p g t", g=G), in_=factor_scale.rearrange("(g p t) o -> p g (t o)", p=P, t=T))
        fb_src = factor_bytes.rearrange("(g p t) n -> p g t n", p=P, t=T)
        psi_src = [psi[v].rearrange("(p t) k -> p t k", t=T) for v in range(V)]

        def load_fb(h, g):
            nc.sync.dma_start(out=fb[h][:, g], in_=fb_src[:, g, :, h * 512:(h + 1) * 512])

        def load_psi(v, t, n=1):
            nc.sync.dma_start(out=psi_raw[v][:, t:t + n, :], in_=psi_src[v][:, t:t + n, :])

        load_psi(0, 0)
        load_fb(0, 0)
        load_fb(0, 1)
        load_psi(0, 1)
        load_psi(0, 2, 2)
        load_psi(1, 0, 2)
        load_psi(1, 2, 2)
        load_fb(1, 0)
        load_fb(1, 1)
        nc.sync.dma_start(out=cum_raw[:], in_=cum.rearrange("(p t) h -> p t h", t=T))
        load_psi(2, 0, 4)
        load_psi(3, 0, 4)

        psi_g = {}
        psi_c = {}
        psi_s = {}
        banks = {}

        def psi_tiles(v):
            psi_g[v] = keep4.tile([P, T, K], BF16, name="psi_g", align_bytes=64)
            psi_c[v] = keep4.tile([P, T, G, P], U32, name="psi_c", align_bytes=64)
            psi_s[v] = keep4.tile([P, T, G, P], U8, name="psi_s", align_bytes=64)

        def psi_transpose(v, t):
            xt = ps_t.tile([P, 4, P], F32, name="xt")
            words = psi_raw[v][:, t, :].bitcast(F32)
            for g in range(G):
                for u in range(2):
                    nc.tensor.transpose(xt[:, 2 * g + u, :], words[:, 256 * g + u:256 * (g + 1):2], ident[:])
            banks[v, t] = xt

        def copy_out(eng, out, in_):
            if eng == "s":
                nc.scalar.copy(out, in_)
            else:
                nc.vector.tensor_copy(out, in_)

        def psi_copy(v, t, eng):
            copy_out(eng, psi_g[v][:, t, :].bitcast(F32).rearrange("p (g r u) -> p g r u", g=G, u=2),
                     banks[v, t][:].rearrange("p (g u) r -> p g r u", g=G))

        def psi_quant(v, t0, n=2):
            nc.vector.quantize_mx(
                out=psi_c[v][:, t0:t0 + n].rearrange("p t g r -> p (t g r)").bitcast(FP8X4),
                scales=psi_s[v][:, t0:t0 + n].rearrange("p t g r -> p (t g r)"),
                in_=psi_g[v][:, t0:t0 + n].rearrange("p t k -> p (t k)"))

        def cum_transpose(b):
            xt = ps_t.tile([P, 4, P], F32, name="xt")
            for i in range(2):
                words = cum_raw[:, 2 * b + i, :].bitcast(F32)
                for u in range(2):
                    nc.tensor.transpose(xt[:, 2 * i + u, :], words[:, u:256:2], ident[:])
            banks["cum", b] = xt

        def cum_copy(b, eng):
            copy_out(eng, cum_g[:, 1024 * b:1024 * (b + 1)].bitcast(F32).rearrange("p (i r u) -> p i r u", i=2, u=2),
                     banks["cum", b][:].rearrange("p (i u) r -> p i r u", i=2))

        def cum_quant():
            nc.vector.quantize_mx(out=cc[:].rearrange("p t r -> p (t r)").bitcast(FP8X4),
                                  scales=cs[:].rearrange("p t r -> p (t r)"), in_=cum_g[:])

        wides = {}
        fgs = {}

        def f_widen(c):
            n = widths[c]
            w = pool.tile([P, G, 2, n, 2], BF16, name="w")
            for g in range(G):
                for t in (0, 2, 1, 3):
                    h, n0 = divmod(starts[c], 512)
                    src = fb[h][:, g, t, n0:n0 + n].bitcast(FP8)
                    sc = fs[:, g * T + t:g * T + t + 1]
                    if (c, g) in CFG["sw"]:
                        flat = w[:, g].rearrange("p b n e -> p (b n e)")
                        nc.scalar.activation(flat[:, t * n:(t + 1) * n], src, ACT.Copy, scale=sc)
                    else:
                        nc.vector.tensor_scalar(w[:, g, t // 2, :, t % 2], src, sc, None, op0=ALU.mult)
            wides[c] = w

        def f_inter(c):
            fg = pool.tile([P, G, widths[c] * T], BF16, name="fg", align_bytes=64)
            for g in sorted(range(G), key=lambda g: (c, g) not in CFG["sw"]):
                if (c, g) in CFG["sw"]:
                    nc.vector.tensor_copy(fg[:, g, :].rearrange("p (n t) -> p n t", t=T),
                                          wides[c][:, g].rearrange("p b n e -> p (b n e)").rearrange("p (t n) -> p n t", t=T))
                else:
                    nc.vector.tensor_copy(fg[:, g, :].bitcast(F32).rearrange("p (n b) -> p n b", b=2),
                                          wides[c][:, g].rearrange("p b n e -> p (b n e)").bitcast(F32).rearrange("p (b n) -> p n b", b=2))
            fgs[c] = fg

        def f_quant(c):
            for g in range(G):
                nc.vector.quantize_mx(out=fc[c][:, g].bitcast(FP8X4), scales=fsc[c][:, g], in_=fgs[c][:, g])

        pw = {}
        pc = {}
        psc = {}
        var = {}
        o = {}
        sums = {}
        recs = {}
        read_done = set()

        def stage1(i):
            v, c = divmod(i, UNITS)
            ps = ps_a.tile([P, T, N_UNIT], F32, name="theta")
            ch = max(x for x in range(len(starts)) if starts[x] <= c * N_UNIT)
            n0 = c * N_UNIT - starts[ch]
            for t in range(T):
                for g in range(G):
                    nc.tensor.matmul_mx(
                        out=ps[:, t, :],
                        lhsT=psi_c[v][:, t, g, :].bitcast(FP8X4), lhsT_scale=psi_s[v][:, t, g, :],
                        rhs=fc[ch][:, g, n0:n0 + N_UNIT].bitcast(FP8X4), rhs_scale=fsc[ch][:, g, n0:n0 + N_UNIT],
                        start=(g == 0), stop=(g == G - 1))
            banks["theta", i] = ps

        def square(i):
            q, a = divmod(i, UNITS_PER_HALF)
            if a == 0:
                pw[q] = pool.tile([P, UNITS_PER_HALF, N_UNIT, T], BF16, name="pw", align_bytes=64)
            nc.scalar.activation(pw[q][:, a], banks["theta", i][:].rearrange("p t n -> p n t"), ACT.Square)

        def pw_quant(q):
            pc[q] = pool.tile([P, HALF], U32, name="pc", align_bytes=64)
            psc[q] = pool.tile([P, HALF], U8, name="psc", align_bytes=64)
            nc.vector.quantize_mx(out=pc[q][:].bitcast(FP8X4), scales=psc[q][:],
                                  in_=pw[q][:].rearrange("p a n t -> p (a n t)"))

        def stage2(q, m):
            ps = ps_b.tile([P, HALF], F32, name="var")
            nc.tensor.matmul_mx(out=ps[:], lhsT=cc[:, m, :].bitcast(FP8X4), lhsT_scale=cs[:, m, :],
                                rhs=pc[q][:].bitcast(FP8X4), rhs_scale=psc[q][:], start=True, stop=True)
            var[q, m] = ps

        def read_var(q, m, eng):
            v, h = divmod(q, 2)
            if h == 0 and m == 0:
                o[v] = outs.tile([P, T, J], F32, name="o")
                sums[v] = outs.tile([P, T, 2], F32, name="sums")
                recs[v] = outs.tile([P, 2, T], F32, name="recs")
            read_done.add((q, m))
            dst = o[v][:, m, h * HALF:(h + 1) * HALF]
            if eng == "s":
                nc.scalar.activation(dst, var[q, m][:], ACT.Copy, accum_out=sums[v][:, m, h:h + 1])
            else:
                nc.vector.tensor_scalar(dst, var[q, m][:], 1.0, None, op0=ALU.mult, op1=ALU.add, accum_out=sums[v][:, m, h:h + 1])

        leveled = set()
        normed = set()

        def lv_red(v, m0, m1):
            leveled.update((v, m) for m in range(m0, m1))
            nc.vector.tensor_reduce(recs[v][:, 0, m0:m1], sums[v][:, m0:m1, :], axis=AX.X, op=ALU.add)

        def lv_rec(v, m0, m1):
            nc.vector.reciprocal(recs[v][:, 1, m0:m1], recs[v][:, 0, m0:m1])

        def levels(v, m0, m1):
            lv_red(v, m0, m1)
            lv_rec(v, m0, m1)

        def norm(v, m):
            normed.add((v, m))
            nc.vector.tensor_scalar(o[v][:, m, :], o[v][:, m, :], recs[v][:, 1, m:m + 1], float(J), op0=ALU.mult, op1=ALU.mult)
            nc.sync.dma_start(out=out[v].rearrange("(p t) n -> p t n", t=T)[:, m, :], in_=o[v][:, m, :])

        for v in range(V):
            psi_tiles(v)
        tr_at = {}
        for key, s in CFG["tr"].items():
            tr_at.setdefault(s, []).append(key)

        def tr(step):
            keys = tr_at.get(step, [])
            for key in keys:
                if key[0] == "cum":
                    cum_transpose(key[1])
                else:
                    psi_transpose(*key)
                e = "v" if key in CFG["cpv"] else "s"
                if key[0] == "cum":
                    cum_copy(key[1], e)
                else:
                    psi_copy(key[0], key[1], e)

        def prep(c):
            f_widen(c)
            f_inter(c)
            f_quant(c)

        f_widen(0)
        for t in range(T):
            psi_transpose(0, t)
            psi_copy(0, t, "s")
        f_inter(0)
        f_quant(0)
        psi_quant(0, 0)
        psi_quant(0, 2)
        for c in range(1, len(widths)):
            if CFG["fstep"][c] == -1:
                prep(c)
        tr(-1)

        n_steps = V * UNITS
        L = CFG["lag2"]
        LR = L + CFG["lagr"]
        for i in range(n_steps + 1):
            v, j = divmod(i, UNITS)
            if i < n_steps:
                stage1(i)
            q, m = divmod(i - LR, 4)
            rd = 0 <= q < 2 * V - 1
            eng = "v" if (q, m) in CFG["rv"] else "s"
            if i < n_steps and CFG["sqf"]:
                square(i)
            if rd and eng == "s":
                read_var(q, m, eng)
            if i < n_steps and not CFG["sqf"]:
                square(i)
            if 1 <= v < V:
                for h in range(2):
                    if CFG["red"][h] == j:
                        lv_red(v - 1, 2 * h, 2 * h + 2)
            if i % 4 == 0 and 4 <= i <= n_steps:
                pw_quant(i // 4 - 1)
            if rd and eng == "v":
                read_var(q, m, eng)
            tr(i)
            for c in range(1, len(widths)):
                if CFG["fstep"][c] == i:
                    prep(c)
            if i == CFG["cq"]:
                cum_quant()
            for w in range(1, V):
                if CFG["pq"][w] == i:
                    psi_quant(w, 0, 4)
            q, m = divmod(i - L, 4)
            if 0 <= q < 2 * V - 1:
                stage2(q, m)
            if 1 <= v < V:
                for h in range(2):
                    if CFG["red"][h] == j:
                        lv_rec(v - 1, 2 * h, 2 * h + 2)
                for m in range(T):
                    if CFG["nm"][m] == j:
                        norm(v - 1, m)
        q7 = 2 * V - 1
        left = [(q7 - 1, m) for m in range(4) if (q7 - 1, m) not in read_done]
        for q, m in left:
            if (q, m) not in var:
                stage2(q, m)
        for q, m in left:
            read_var(q, m, "v")
        for m in range(T):
            stage2(q7, m)
        read_var(q7, 0, "s")
        read_var(q7, 1, "v")
        read_var(q7, 2, "s")
        read_var(q7, 3, "s")
        lv_red(V - 1, 0, 1)
        lv_red(V - 1, 1, 2)
        lv_rec(V - 1, 0, 1)
        lv_rec(V - 1, 1, 2)
        norm(V - 1, 0)
        lv_red(V - 1, 2, 4)
        norm(V - 1, 1)
        lv_rec(V - 1, 2, 4)
        norm(V - 1, 2)
        norm(V - 1, 3)
